import numpy as np
import ml_dtypes


def mxq(x, axis, fmt="e4m3"):
    dtype, down = {"e4m3": (ml_dtypes.float8_e4m3fn, 7), "e5m2": (ml_dtypes.float8_e5m2, 14)}[fmt]
    v = np.moveaxis(np.asarray(x, np.float32).astype(ml_dtypes.bfloat16).astype(np.float64), axis, -1)
    blocks = v.reshape(v.shape[:-1] + (-1, 32))
    amax = np.abs(blocks).max(-1, keepdims=True)
    byte = np.maximum(np.where(amax > 0, np.frexp(amax)[1] - 1 + 127, 0) - down, 1)
    scale = np.exp2(byte - 127.0)
    codes = (blocks / scale).astype(np.float32).astype(dtype).astype(np.float64)
    return np.moveaxis((codes * scale).reshape(v.shape), -1, axis)


WIDE = False


def mx_kscale(k):
    if not WIDE:
        return np.ones(k)
    levels = np.array([10, -10, 5, -5, 0])
    if k % 512:
        return np.exp2(np.random.permutation(np.resize(levels, k // 32))).repeat(32)
    a = np.empty((k // 512, 16))
    for p in range(k // 512):
        a[p, :8] = np.random.permutation(np.resize(levels, 8))
        for g in range(8):
            far = levels[np.abs(levels - a[p, g]) >= 10]
            a[p, g + 8] = far[np.random.randint(len(far))]
    return np.exp2(a.ravel()).repeat(32)


def f64(x):
    return np.asarray(x).astype(np.float64)


def striped(idx):
    return np.tile(idx.reshape(-1, 16).T, (8, 1)).astype(np.uint16)


def unstriped(offs):
    return offs[:16].T.reshape(-1).astype(np.int64)


def pack_weight(w):
    k, n = w.shape
    w = f64(np.asarray(w, np.float32).astype(ml_dtypes.bfloat16)).reshape(k // 32, 32, n)
    amax = np.abs(w).max(1)
    byte = np.clip(np.where(amax > 0, np.frexp(amax)[1] - 1 + 127 - 7, 1), 1, 254)
    scaled = (w * np.exp2(127.0 - byte)[:, None, :]).reshape(k, n).astype(np.float32)
    words = np.ascontiguousarray(scaled.reshape(k // 512, 128, 4, n).transpose(0, 1, 3, 2)).astype(ml_dtypes.float8_e4m3fn).view(np.uint8)
    return words, np.ascontiguousarray(byte.astype(np.uint8).reshape(k // 512, 16, n))


def unpack_weight(words, scales):
    g, p, n, _ = words.shape
    vals = np.ascontiguousarray(words).view(ml_dtypes.float8_e4m3fn).astype(np.float64) * np.repeat(np.exp2(scales.astype(np.float64) - 127.0), 8, axis=1)[..., None]
    return vals.transpose(0, 1, 3, 2).reshape(g * 512, n)


K, T, S, D, H, Z, W = 512, 2048, 512, 2, 512, 512, 2048
P = 2 ** 7


def setup_inputs():
    n = np.random.standard_normal
    s = mx_kscale(K)[:, None]
    packed_xT = pack_weight(n((K, T)) * s)
    packed_eT = pack_weight(n((K, W)) * s)
    return {
        "x_words": packed_xT[0],
        "x_scales": packed_xT[1],
        "w1": (n((K, H)) / np.sqrt(K) / s).astype(np.float32),
        "w2": (n((K, H)) / np.sqrt(K) / s).astype(np.float32),
        "e_words": packed_eT[0],
        "e_scales": packed_eT[1],
        "unit": (np.random.uniform(0.6, 1.4, (K, 1)) / np.sqrt(K) / s).astype(np.float32),
        "mth": (np.tile(np.random.uniform(0.3, 1.3, W), (P, 1))).astype(np.float32),
        "offs": striped(np.random.permutation(T)[:S]),
        "syn": striped(np.random.permutation(S)),
        "adk": striped(np.random.permutation(W)[:Z]),
        "brd": striped(np.random.permutation(Z)),
    }


def reference(x_words, x_scales, w1, w2, e_words, e_scales, unit, mth, offs, syn, adk, brd):
    xq = unpack_weight(x_words, x_scales)[:, unstriped(offs)]
    y = mxq(f64(w1), 0, "e4m3").T @ xq
    yg = mxq(f64(w2), 0, "e4m3").T @ xq
    gs = yg[:, unstriped(syn)]
    bst = np.maximum(y, gs)
    aw = bst * np.abs(y)
    qv = aw.reshape(len(aw), -1, D).sum(axis=2)
    sat = qv / (np.sqrt((qv) ** 2 + 0.5))
    hid = f64(unit) * sat
    e_adk = unpack_weight(e_words, e_scales)[:, unstriped(adk)]
    sc = mxq(hid, 0, "e4m3").T @ e_adk
    grp4 = sc.reshape(len(sc), -1, 4).mean(axis=2)
    excl = sc - (0.8 * np.repeat(grp4, 4, axis=1))
    xm = excl * (f64(mth)[:1][:, unstriped(adk)])
    return np.minimum(xm, excl[:, unstriped(brd)])

@@ -1,0 +1,278 @@
+from contextlib import ExitStack
+
+import concourse.mybir as mybir
+from concourse.masks import make_identity
+
+F32 = mybir.dt.float32
+BF16 = mybir.dt.bfloat16
+I32 = mybir.dt.int32
+U32 = mybir.dt.uint32
+U16 = mybir.dt.uint16
+U8 = mybir.dt.uint8
+FP8X4 = mybir.dt.float8_e4m3fn_x4
+ALU = mybir.AluOpType
+ACT = mybir.ActivationFunctionType
+
+P = 128
+PACK = 4
+K, T, S, H, Z = 512, 2048, 512, 512, 512
+V = S // 2
+HALF = S // 2
+FLOPS = 2 * (2 * K * H * S + H * V * Z)
+
+
+def tile_picked_ysponsq_min_p_kernel(
+    tc, x_words, x_scales, w1, w2, e_words, e_scales, unit, mth, offs, syn, adk, brd, out
+):
+    nc = tc.nc
+    with ExitStack() as ctx:
+        sb = ctx.enter_context(tc.tile_pool(name="sb", bufs=1))
+        ps = ctx.enter_context(tc.psum_pool(name="ps", bufs=1))
+
+        def load_list(name, src):
+            lst = sb.tile([P, S // 16], U16, name=name)
+            nc.sync.dma_start(lst[:], src)
+            return lst
+
+        def load_words(name, src):
+            words = sb.tile([P, T], I32, name=name)
+            nc.sync.dma_start(words[:], src[0].rearrange("p n t -> p (n t)").bitcast(I32))
+            return words
+
+        def load_scales(name, src, clear, queue):
+            plane = sb.tile([P, T], U8, name=name)
+            clear.memset(plane[:].bitcast(I32), 0)
+            rows = src[0].bitcast(I32)
+            for r in range(4):
+                queue.dma_start(plane[r:P:32, :].bitcast(I32), rows[r:16:4, :])
+            return plane
+
+        def load_weight(name, src, half):
+            raw = sb.tile([P, PACK, H // 2], F32, name=name)
+            cols = slice(half * H // 2, (half + 1) * H // 2)
+            nc.sync.dma_start(raw[:], src.rearrange("(p j) c -> p j c", j=PACK)[:, :, cols])
+            return raw
+
+        def gather_words(name, table, lst, tag):
+            picked = sb.tile([P, lst.shape[1] * 16], U32, name=name, tag=tag, align_bytes=64)
+            nc.vector.tensor_copy(picked[:], table[:].bitcast(U32).indirect(lst))
+            return picked[:]
+
+        def gather_scales(name, table, lst, tag):
+            picked = sb.tile([P, S], U8, name=name, tag=tag, align_bytes=64)
+            nc.vector.tensor_copy(picked[:], table[:].indirect(lst))
+            return picked[:]
+
+        def round_weight(name, raw, cols, copy):
+            part = raw[:, :, cols]
+            grouped = sb.tile([P, part.shape[2], PACK], BF16, name=name, align_bytes=64)
+            copy(
+                grouped[:].rearrange("p (c i) j -> p c j i", i=4),
+                part.rearrange("p j (c i) -> p c j i", i=4),
+            )
+            return grouped
+
+        def quantize(name, grouped):
+            width = grouped.shape[1]
+            codes = sb.tile([P, width], U32, name=name + "_codes", align_bytes=64)
+            scales = sb.tile([P, width], U8, name=name + "_scales", align_bytes=64)
+            nc.vector.quantize_mx(
+                out=codes[:].bitcast(FP8X4),
+                scales=scales[:],
+                in_=grouped[:].rearrange("p c j -> p (c j)"),
+            )
+            return codes, scales
+
+        def product(acc, stationary, rows, moving, cols):
+            nc.tensor.matmul_mx(
+                out=acc,
+                lhsT=stationary[0][:, rows].bitcast(FP8X4),
+                lhsT_scale=stationary[1][:, rows],
+                rhs=moving[0][:, cols].bitcast(FP8X4),
+                rhs_scale=moving[1][:, cols],
+                start=True,
+                stop=True,
+            )
+
+        offs_t = load_list("offs_t", offs)
+        w2_raw = [load_weight("w2_raw0", w2, 0)]
+        xs_table = load_scales("xs_table", x_scales, nc.gpsimd, nc.sync)
+        x_table = load_words("x_table", x_words)
+        ident = sb.tile([P, P], F32, name="ident")
+        make_identity(nc, ident[:])
+        w1_raw = [load_weight("w1_raw0", w1, 0)]
+        syn_t = load_list("syn_t", syn)
+        w2_raw.append(load_weight("w2_raw1", w2, 1))
+        w1_raw.append(load_weight("w1_raw1", w1, 1))
+        adk_t = load_list("adk_t", adk)
+        unit_t = sb.tile([P, PACK], F32, name="unit_t")
+        nc.sync.dma_start(unit_t[:], unit.rearrange("(p t) o -> p (t o)", t=PACK))
+        es_table = load_scales("es_table", e_scales, nc.vector, nc.sync)
+        e_table = load_words("e_table", e_words)
+        brd_t = load_list("brd_t", brd)
+        mth_t = sb.tile([P, T], F32, name="mth_t")
+        nc.sync.dma_start(mth_t[:], mth)
+
+        first, second, both = slice(0, P), slice(P, 2 * P), slice(0, 2 * P)
+        y_ps, yg_sb = [], []
+
+        def project_synonym(a, w_q, rows):
+            yg_ps = ps.tile([P, S], F32, name=f"yg_ps{a}", tag="turn", bufs=2)
+            for h in range(2):
+                product(yg_ps[:, h * HALF : (h + 1) * HALF], w_q, rows, x_pick[h], both)
+            yg_sb.append(sb.tile([P, S], F32, name=f"yg_sb{a}", tag=f"yg_sb{a}"))
+            nc.scalar.copy(yg_sb[a][:], yg_ps[:])
+
+        def project_keyword(a, w_q, rows):
+            y_ps.append(ps.tile([P, S], F32, name=f"y_ps{a}", tag=f"y_bank{a}"))
+            for h in range(2):
+                product(y_ps[a][:, h * HALF : (h + 1) * HALF], w_q, rows, x_pick[h], both)
+
+        def look_up(a, h, tag, mag_tag):
+            gs = sb.tile([P, HALF], F32, name=f"gs{a}{h}", tag=tag)
+            nc.scalar.activation(
+                gs[:], yg_sb[a][:].indirect(syn_t[:, h * 16 : (h + 1) * 16]), ACT.Copy
+            )
+            mag = sb.tile([P, HALF], F32, name=f"mag{a}{h}", tag=mag_tag)
+            nc.scalar.activation(mag[:], y_ps[a][:, h * HALF : (h + 1) * HALF], ACT.Abs)
+            return gs, mag
+
+        def best(a, h, gs):
+            bst = sb.tile([P, HALF], F32, name=f"bst{a}{h}", tag=f"bst{a}{h}", align_bytes=64)
+            nc.vector.tensor_tensor(bst[:], y_ps[a][:, h * HALF : (h + 1) * HALF], gs[:], ALU.max)
+            return bst
+
+        def weigh(a, h, bst, mag, q_cols):
+            aw = sb.tile([P, HALF], F32, name=f"aw{a}{h}")
+            nc.vector.tensor_tensor(aw[:], bst[:], mag[:], ALU.mult)
+            for d in range(2):
+                nc.tensor.matmul(
+                    q_cols, aw[:, d:HALF:2], ident[:], start=(d == 0), stop=(d == 1), is_transpose=True
+                )
+
+        def inverse_norm(name, q_t, tag):
+            width = q_t.shape[1] // PACK
+            sq = sb.tile([P, PACK, width], F32, name="sq" + name, tag=tag)
+            nc.scalar.activation(sq[:], q_t.rearrange("v (p t) -> v t p", t=PACK), ACT.Square)
+            rs = sb.tile([P, PACK, width], F32, name="rs" + name)
+            nc.scalar.activation(rs[:], sq[:], ACT.Abs_reciprocal_sqrt, bias=0.5)
+            return rs
+
+        def saturate(sat_cols, q_t, rs):
+            nc.vector.tensor_tensor(
+                sat_cols, q_t.rearrange("v (p t) -> v t p", t=PACK), rs[:], ALU.mult
+            )
+
+        def turn_back(h, sat):
+            sat_t = ps.tile([P, PACK, P], F32, name=f"sat_t{h}", tag="turn", bufs=2)
+            for t in range(PACK):
+                nc.tensor.transpose(sat_t[:, t, :], sat[:, t, :], ident[:])
+            return sat_t
+
+        def hidden(h, sat_t):
+            hid = sb.tile([P, P, PACK], BF16, name=f"hid{h}", align_bytes=64)
+            nc.vector.tensor_tensor(
+                hid[:],
+                sat_t[:].rearrange("p t v -> p v t"),
+                unit_t[:].unsqueeze(1).to_broadcast([P, P, PACK]),
+                ALU.mult,
+            )
+            return hid
+
+        def score(h, hid):
+            hid_q = quantize(f"hid_q{h}", hid)
+            sc = []
+            for c in range(2):
+                sc.append(ps.tile([P, Z // 2], F32, name=f"sc{h}{c}", tag=f"y_bank{2 * h + c}"))
+                product(sc[c][:], hid_q, first, e_pick, slice(c * Z // 2, (c + 1) * Z // 2))
+            return sc
+
+        def exclude(h, sc):
+            total = sb.tile([P, 2, Z // 8], F32, name=f"total{h}")
+            excl = sb.tile([P, Z], F32, name=f"excl{h}")
+            groups = [sc[c][:].rearrange("v (z d) -> v z d", d=4) for c in range(2)]
+            for c in range(2):
+                nc.vector.tensor_reduce(total[:, c, :], groups[c], mybir.AxisListType.X, ALU.add)
+            for c in range(2):
+                nc.vector.scalar_tensor_tensor(
+                    excl[:, c * Z // 2 : (c + 1) * Z // 2].rearrange("v (z d) -> v z d", d=4),
+                    total[:, c, :].unsqueeze(2).to_broadcast([P, Z // 8, 4]),
+                    -0.8 / 4,
+                    groups[c],
+                    ALU.mult,
+                    ALU.add,
+                )
+            return excl
+
+        def finish(h, excl):
+            broad = []
+            for c in range(2):
+                broad.append(sb.tile([P, Z // 2], F32, name=f"broad{h}{c}"))
+                nc.scalar.activation(
+                    broad[c][:], excl[:].indirect(brd_t[:, c * 16 : (c + 1) * 16]), ACT.Copy
+                )
+            xm = sb.tile([P, Z], F32, name=f"xm{h}")
+            nc.vector.tensor_tensor(xm[:], excl[:], strict[:], ALU.mult)
+            for c in range(2):
+                cols = slice(c * Z // 2, (c + 1) * Z // 2)
+                res = sb.tile([P, Z // 2], F32, name=f"res{h}{c}")
+                nc.vector.tensor_tensor(res[:], xm[:, cols], broad[c][:], ALU.min)
+                nc.sync.dma_start(out[h * P : (h + 1) * P, cols], res[:])
+
+        on_vector = nc.vector.tensor_copy
+        w2_bf = round_weight("w2_bf0", w2_raw[0], both, nc.scalar.copy)
+        xs_pick = gather_scales("xs_pick", xs_table, offs_t[:], "xs_pick")
+        w2_q = quantize("w2_q0", w2_bf)
+        x_pick = [
+            (gather_words(f"x_pick{h}", x_table, offs_t[:, h * 16 : (h + 1) * 16], f"x_pick{h}"), xs_pick[:, h * HALF : (h + 1) * HALF])
+            for h in range(2)
+        ]
+        project_synonym(0, w2_q, first)
+        project_synonym(1, w2_q, second)
+        w1_bf = [round_weight(f"w1_bf{a}", w1_raw[0], (first, second)[a], on_vector) for a in range(2)]
+        project_keyword(0, quantize("w1_q0", w1_bf[0]), first)
+        project_keyword(1, quantize("w1_q1", w1_bf[1]), first)
+        q0 = ps.tile([P, H], F32, name="q0", tag="q_bank0")
+        found = [look_up(a, 0, f"gs{a}0", f"mag{a}0") for a in (0, 1)]
+        w2_q = quantize("w2_q2", round_weight("w2_bf2", w2_raw[1], both, on_vector))
+        w1_q = quantize("w1_q2", round_weight("w1_bf2", w1_raw[1], both, on_vector))
+        for a in (2, 3):
+            project_synonym(a, w2_q, (first, second)[a - 2])
+            project_keyword(a, w1_q, (first, second)[a - 2])
+            found.append(look_up(a, 0, f"gs{a}0", f"mag{a}0"))
+        for pair in ((0, 1), (2, 3)):
+            bst = [best(a, 0, found[a][0]) for a in pair]
+            for a, b in zip(pair, bst):
+                weigh(a, 0, b, found[a][1], q0[:, a * P : (a + 1) * P])
+
+        found = [look_up(0, 1, "gs20", "mag20")]
+        rs0 = inverse_norm("0", q0[:], "sq0")
+        found.append(look_up(1, 1, "sq0", "mag30"))
+        es_pick = gather_scales("es_pick", es_table, adk_t[:], "bst20")
+        e_pick = (gather_words("e_pick", e_table, adk_t[:], "bst30"), es_pick)
+        sat0 = sb.tile([P, PACK, P], F32, name="sat0")
+        saturate(sat0[:], q0[:], rs0)
+        sat_t0 = turn_back(0, sat0)
+        q1 = [ps.tile([P, H // 2], F32, name="q1a", tag="q_bank1")]
+        bst = [best(a, 1, found[a][0]) for a in (0, 1)]
+        for a in (0, 1):
+            weigh(a, 1, bst[a], found[a][1], q1[0][:, a * P : (a + 1) * P])
+        hid0 = hidden(0, sat_t0)
+        found.extend([look_up(a, 1, ("gs20", "sq0")[a - 2], ("mag20", "mag30")[a - 2]) for a in (2, 3)])
+        sc0 = score(0, hid0)
+        q1.append(ps.tile([P, H // 2], F32, name="q1b", tag="q_bank0"))
+        bst = [best(a, 1, found[a][0]) for a in (2, 3)]
+        for a in (0, 1):
+            weigh(a + 2, 1, bst[a], found[a + 2][1], q1[1][:, a * P : (a + 1) * P])
+        rs1 = [inverse_norm("1a", q1[0][:], "sq1a")]
+        strict = sb.tile([P, Z], F32, name="strict", tag="yg_sb3")
+        nc.scalar.activation(strict[:], mth_t[:].indirect(adk_t[:]), ACT.Copy)
+        rs1.append(inverse_norm("1b", q1[1][:], "sq1b"))
+        excl0 = exclude(0, sc0)
+        sat1 = sb.tile([P, PACK, P], F32, name="sat1")
+        for r in range(2):
+            saturate(sat1[:, :, r * P // 2 : (r + 1) * P // 2], q1[r][:], rs1[r])
+        hid1 = hidden(1, turn_back(1, sat1))
+        sc1 = score(1, hid1)
+        finish(0, excl0)
+        finish(1, exclude(1, sc1))

@@ -47,10 +47,9 @@ def tile_picked_ysponsq_min_p_kernel(
                 queue.dma_start(plane[r:P:32, :].bitcast(I32), rows[r:16:4, :])
             return plane
 
-        def load_weight(name, src, half):
-            raw = sb.tile([P, PACK, H // 2], F32, name=name)
-            cols = slice(half * H // 2, (half + 1) * H // 2)
-            nc.sync.dma_start(raw[:], src.rearrange("(p j) c -> p j c", j=PACK)[:, :, cols])
+        def load_weight(name, src, lo, hi):
+            raw = sb.tile([P, PACK, hi - lo], F32, name=name)
+            nc.sync.dma_start(raw[:], src.rearrange("(p j) c -> p j c", j=PACK)[:, :, lo:hi])
             return raw
 
         def gather_words(name, table, lst, tag):
@@ -63,9 +62,9 @@ def tile_picked_ysponsq_min_p_kernel(
             nc.vector.tensor_copy(picked[:], table[:].indirect(lst))
             return picked[:]
 
-        def round_weight(name, raw, cols, copy):
+        def round_weight(name, raw, cols, copy, tag=None):
             part = raw[:, :, cols]
-            grouped = sb.tile([P, part.shape[2], PACK], BF16, name=name, align_bytes=64)
+            grouped = sb.tile([P, part.shape[2], PACK], BF16, name=name, tag=tag or name, align_bytes=64)
             copy(
                 grouped[:].rearrange("p (c i) j -> p c j i", i=4),
                 part.rearrange("p j (c i) -> p c j i", i=4),
@@ -94,79 +93,96 @@ def tile_picked_ysponsq_min_p_kernel(
                 stop=True,
             )
 
+        warm = sb.tile([P, 1], F32, name="warm")
+        nc.vector.memset(warm[:], 1.0)
+        warm_out = sb.tile([P, 1], F32, name="warm_out")
+        nc.scalar.activation(warm_out[:], warm[:], ACT.Abs_reciprocal_sqrt)
         offs_t = load_list("offs_t", offs)
-        w2_raw = [load_weight("w2_raw0", w2, 0)]
+        w2_a0 = load_weight("w2_a0", w2, 0, P)
         xs_table = load_scales("xs_table", x_scales, nc.gpsimd, nc.sync)
         x_table = load_words("x_table", x_words)
         ident = sb.tile([P, P], F32, name="ident")
         make_identity(nc, ident[:])
-        w1_raw = [load_weight("w1_raw0", w1, 0)]
+        w1_a0 = load_weight("w1_a0", w1, 0, P)
         syn_t = load_list("syn_t", syn)
-        w2_raw.append(load_weight("w2_raw1", w2, 1))
-        w1_raw.append(load_weight("w1_raw1", w1, 1))
+        w2_a1 = load_weight("w2_a1", w2, P, 2 * P)
+        w1_a1 = load_weight("w1_a1", w1, P, 2 * P)
+        w2_hi = load_weight("w2_hi", w2, 2 * P, H)
+        w1_hi = load_weight("w1_hi", w1, 2 * P, H)
         adk_t = load_list("adk_t", adk)
-        unit_t = sb.tile([P, PACK], F32, name="unit_t")
-        nc.sync.dma_start(unit_t[:], unit.rearrange("(p t) o -> p (t o)", t=PACK))
         es_table = load_scales("es_table", e_scales, nc.vector, nc.sync)
         e_table = load_words("e_table", e_words)
+        unit_t = sb.tile([P, PACK], F32, name="unit_t")
+        nc.sync.dma_start(unit_t[:], unit.rearrange("(p t) o -> p (t o)", t=PACK))
         brd_t = load_list("brd_t", brd)
         mth_t = sb.tile([P, T], F32, name="mth_t")
         nc.sync.dma_start(mth_t[:], mth)
 
         first, second, both = slice(0, P), slice(P, 2 * P), slice(0, 2 * P)
-        y_ps, yg_sb = [], []
+        y_ps, yg_ps, yg_sb, mag, gs, bst = {}, {}, {}, {}, {}, {}
+        halves = [slice(h * HALF, (h + 1) * HALF) for h in range(2)]
+
+        def project(acc, w_q, rows):
+            for h in range(2):
+                product(acc[:, halves[h]], w_q, rows, x_pick[h], both)
 
         def project_synonym(a, w_q, rows):
-            yg_ps = ps.tile([P, S], F32, name=f"yg_ps{a}", tag="turn", bufs=2)
-            for h in range(2):
-                product(yg_ps[:, h * HALF : (h + 1) * HALF], w_q, rows, x_pick[h], both)
-            yg_sb.append(sb.tile([P, S], F32, name=f"yg_sb{a}", tag=f"yg_sb{a}"))
-            nc.scalar.copy(yg_sb[a][:], yg_ps[:])
+            yg_ps[a] = ps.tile([P, S], F32, name=f"yg_ps{a}", tag="turn", bufs=2)
+            project(yg_ps[a], w_q, rows)
 
         def project_keyword(a, w_q, rows):
-            y_ps.append(ps.tile([P, S], F32, name=f"y_ps{a}", tag=f"y_bank{a}"))
+            y_ps[a] = ps.tile([P, S], F32, name=f"y_ps{a}", tag="y_bank", bufs=3)
+            project(y_ps[a], w_q, rows)
+
+        def empty(a, copy):
+            yg_sb[a] = sb.tile([P, S], F32, name=f"yg_sb{a}")
+            copy(yg_sb[a][:], yg_ps[a][:])
+
+        def magnitude(a):
+            mag[a] = sb.tile([P, S], F32, name=f"mag{a}")
+            nc.scalar.activation(mag[a][:], y_ps[a][:], ACT.Abs)
+
+        def look_up(a):
+            gs[a] = sb.tile([P, S], F32, name=f"gs{a}")
             for h in range(2):
-                product(y_ps[a][:, h * HALF : (h + 1) * HALF], w_q, rows, x_pick[h], both)
+                window = yg_sb[a][:].indirect(syn_t[:, h * 16 : (h + 1) * 16])
+                nc.scalar.activation(gs[a][:, halves[h]], window, ACT.Copy)
 
-        def look_up(a, h, tag, mag_tag):
-            gs = sb.tile([P, HALF], F32, name=f"gs{a}{h}", tag=tag)
-            nc.scalar.activation(
-                gs[:], yg_sb[a][:].indirect(syn_t[:, h * 16 : (h + 1) * 16]), ACT.Copy
-            )
-            mag = sb.tile([P, HALF], F32, name=f"mag{a}{h}", tag=mag_tag)
-            nc.scalar.activation(mag[:], y_ps[a][:, h * HALF : (h + 1) * HALF], ACT.Abs)
-            return gs, mag
-
-        def best(a, h, gs):
-            bst = sb.tile([P, HALF], F32, name=f"bst{a}{h}", tag=f"bst{a}{h}", align_bytes=64)
-            nc.vector.tensor_tensor(bst[:], y_ps[a][:, h * HALF : (h + 1) * HALF], gs[:], ALU.max)
+        def best(a, cols, tag):
+            bst = sb.tile([P, cols.stop - cols.start], F32, name=f"bst{a}_{cols.start}", tag=tag, align_bytes=64)
+            nc.vector.tensor_tensor(bst[:], y_ps[a][:, cols], gs[a][:, cols], ALU.max)
             return bst
 
-        def weigh(a, h, bst, mag, q_cols):
-            aw = sb.tile([P, HALF], F32, name=f"aw{a}{h}")
-            nc.vector.tensor_tensor(aw[:], bst[:], mag[:], ALU.mult)
-            for d in range(2):
-                nc.tensor.matmul(
-                    q_cols, aw[:, d:HALF:2], ident[:], start=(d == 0), stop=(d == 1), is_transpose=True
-                )
+        def weigh(a, cols, bst, engine):
+            aw = sb.tile([P, cols.stop - cols.start], F32, name=f"aw{a}_{cols.start}")
+            engine.tensor_tensor(aw[:], bst[:], mag[a][:, cols], ALU.mult)
+            n = max(a - 1, 0)
+            col = (a - groups[n][0]) * P
+            for lo in range(0, cols.stop - cols.start, HALF):
+                for d in range(2):
+                    nc.tensor.matmul(
+                        q_bank[n][:, (cols.start + lo) // HALF, col : col + P],
+                        aw[:, lo + d : lo + HALF : 2],
+                        ident[:],
+                        start=(d == 0),
+                        stop=(d == 1),
+                        is_transpose=True,
+                    )
 
-        def inverse_norm(name, q_t, tag):
-            width = q_t.shape[1] // PACK
-            sq = sb.tile([P, PACK, width], F32, name="sq" + name, tag=tag)
-            nc.scalar.activation(sq[:], q_t.rearrange("v (p t) -> v t p", t=PACK), ACT.Square)
-            rs = sb.tile([P, PACK, width], F32, name="rs" + name)
+        def square(name, dealt):
+            sq = sb.tile(list(dealt.shape), F32, name="sq" + name, tag="sq" + name)
+            nc.scalar.activation(sq[:], dealt, ACT.Square)
+            return sq
+
+        def inverse_root(name, sq):
+            rs = sb.tile(list(sq.shape), F32, name="rs" + name, tag="rs" + name, align_bytes=64)
             nc.scalar.activation(rs[:], sq[:], ACT.Abs_reciprocal_sqrt, bias=0.5)
             return rs
-
-        def saturate(sat_cols, q_t, rs):
-            nc.vector.tensor_tensor(
-                sat_cols, q_t.rearrange("v (p t) -> v t p", t=PACK), rs[:], ALU.mult
-            )
 
         def turn_back(h, sat):
             sat_t = ps.tile([P, PACK, P], F32, name=f"sat_t{h}", tag="turn", bufs=2)
             for t in range(PACK):
-                nc.tensor.transpose(sat_t[:, t, :], sat[:, t, :], ident[:])
+                nc.tensor.transpose(sat_t[:, t, :], sat[:, h, t, :], ident[:])
             return sat_t
 
         def hidden(h, sat_t):
@@ -183,7 +199,7 @@ def tile_picked_ysponsq_min_p_kernel(
             hid_q = quantize(f"hid_q{h}", hid)
             sc = []
             for c in range(2):
-                sc.append(ps.tile([P, Z // 2], F32, name=f"sc{h}{c}", tag=f"y_bank{2 * h + c}"))
+                sc.append(ps.tile([P, Z // 2], F32, name=f"sc{h}{c}", tag=("y_bank", "y_bank", "y_bank", "q_bank0")[2 * h + c], bufs=(3, 3, 3, 1)[2 * h + c]))
                 product(sc[c][:], hid_q, first, e_pick, slice(c * Z // 2, (c + 1) * Z // 2))
             return sc
 
@@ -204,75 +220,90 @@ def tile_picked_ysponsq_min_p_kernel(
                 )
             return excl
 
-        def finish(h, excl):
-            broad = []
+        def broader(h, excl):
+            broad = sb.tile([P, Z], F32, name=f"broad{h}")
             for c in range(2):
-                broad.append(sb.tile([P, Z // 2], F32, name=f"broad{h}{c}"))
                 nc.scalar.activation(
-                    broad[c][:], excl[:].indirect(brd_t[:, c * 16 : (c + 1) * 16]), ACT.Copy
+                    broad[:, halves[c]], excl[:].indirect(brd_t[:, c * 16 : (c + 1) * 16]), ACT.Copy
                 )
+            return broad
+
+        def scaled(h, excl, engine):
             xm = sb.tile([P, Z], F32, name=f"xm{h}")
-            nc.vector.tensor_tensor(xm[:], excl[:], strict[:], ALU.mult)
-            for c in range(2):
-                cols = slice(c * Z // 2, (c + 1) * Z // 2)
-                res = sb.tile([P, Z // 2], F32, name=f"res{h}{c}")
-                nc.vector.tensor_tensor(res[:], xm[:, cols], broad[c][:], ALU.min)
+            engine.tensor_tensor(xm[:], excl[:], strict[:], ALU.mult)
+            return xm
+
+        def finish(h, xm, broad, parts):
+            for n, cols in enumerate(parts):
+                res = sb.tile([P, cols.stop - cols.start], F32, name=f"res{h}{n}")
+                nc.vector.tensor_tensor(res[:], xm[:, cols], broad[:, cols], ALU.min)
                 nc.sync.dma_start(out[h * P : (h + 1) * P, cols], res[:])
 
-        on_vector = nc.vector.tensor_copy
-        w2_bf = round_weight("w2_bf0", w2_raw[0], both, nc.scalar.copy)
+        on_vector, on_scalar = nc.vector.tensor_copy, nc.scalar.copy
+        w2_bf = [round_weight("w2_bf0", w2_a0, first, on_scalar)]
         xs_pick = gather_scales("xs_pick", xs_table, offs_t[:], "xs_pick")
-        w2_q = quantize("w2_q0", w2_bf)
+        w2_q0 = quantize("w2_q0", w2_bf[0])
         x_pick = [
             (gather_words(f"x_pick{h}", x_table, offs_t[:, h * 16 : (h + 1) * 16], f"x_pick{h}"), xs_pick[:, h * HALF : (h + 1) * HALF])
             for h in range(2)
         ]
-        project_synonym(0, w2_q, first)
-        project_synonym(1, w2_q, second)
-        w1_bf = [round_weight(f"w1_bf{a}", w1_raw[0], (first, second)[a], on_vector) for a in range(2)]
-        project_keyword(0, quantize("w1_q0", w1_bf[0]), first)
-        project_keyword(1, quantize("w1_q1", w1_bf[1]), first)
-        q0 = ps.tile([P, H], F32, name="q0", tag="q_bank0")
-        found = [look_up(a, 0, f"gs{a}0", f"mag{a}0") for a in (0, 1)]
-        w2_q = quantize("w2_q2", round_weight("w2_bf2", w2_raw[1], both, on_vector))
-        w1_q = quantize("w1_q2", round_weight("w1_bf2", w1_raw[1], both, on_vector))
-        for a in (2, 3):
-            project_synonym(a, w2_q, (first, second)[a - 2])
-            project_keyword(a, w1_q, (first, second)[a - 2])
-            found.append(look_up(a, 0, f"gs{a}0", f"mag{a}0"))
-        for pair in ((0, 1), (2, 3)):
-            bst = [best(a, 0, found[a][0]) for a in pair]
-            for a, b in zip(pair, bst):
-                weigh(a, 0, b, found[a][1], q0[:, a * P : (a + 1) * P])
+        every = slice(0, S)
+        groups = ((0, 1), (2,), (3,))
+        q_bank = [ps.tile([P, 2, len(g) * P], F32, name=f"q_bank{n}", tag=f"q_bank{n}") for n, g in enumerate(groups)]
+        dealt = [q[:].rearrange("v h (p t) -> v h t p", t=PACK) for q in q_bank]
+        rs = {}
 
-        found = [look_up(0, 1, "gs20", "mag20")]
-        rs0 = inverse_norm("0", q0[:], "sq0")
-        found.append(look_up(1, 1, "sq0", "mag30"))
-        es_pick = gather_scales("es_pick", es_table, adk_t[:], "bst20")
-        e_pick = (gather_words("e_pick", e_table, adk_t[:], "bst30"), es_pick)
-        sat0 = sb.tile([P, PACK, P], F32, name="sat0")
-        saturate(sat0[:], q0[:], rs0)
-        sat_t0 = turn_back(0, sat0)
-        q1 = [ps.tile([P, H // 2], F32, name="q1a", tag="q_bank1")]
-        bst = [best(a, 1, found[a][0]) for a in (0, 1)]
-        for a in (0, 1):
-            weigh(a, 1, bst[a], found[a][1], q1[0][:, a * P : (a + 1) * P])
-        hid0 = hidden(0, sat_t0)
-        found.extend([look_up(a, 1, ("gs20", "sq0")[a - 2], ("mag20", "mag30")[a - 2]) for a in (2, 3)])
-        sc0 = score(0, hid0)
-        q1.append(ps.tile([P, H // 2], F32, name="q1b", tag="q_bank0"))
-        bst = [best(a, 1, found[a][0]) for a in (2, 3)]
-        for a in (0, 1):
-            weigh(a + 2, 1, bst[a], found[a + 2][1], q1[1][:, a * P : (a + 1) * P])
-        rs1 = [inverse_norm("1a", q1[0][:], "sq1a")]
-        strict = sb.tile([P, Z], F32, name="strict", tag="yg_sb3")
+        def saturate(n):
+            lo, hi = groups[n][0] * P // PACK, (groups[n][-1] + 1) * P // PACK
+            nc.vector.tensor_tensor(sat[:, :, :, lo:hi], dealt[n], rs[n][:], ALU.mult)
+
+        sat = sb.tile([P, 2, PACK, P], F32, name="sat")
+        project_synonym(0, w2_q0, first)
+        w1_bf0 = round_weight("w1_bf0", w1_a0, first, on_scalar)
+        empty(0, on_scalar)
+        w2_bf1 = round_weight("w2_bf1", w2_a1, first, on_vector)
+        project_keyword(0, quantize("w1_q0", w1_bf0), first)
+        project_synonym(1, quantize("w2_q1", w2_bf1), first)
+        w1_bf1 = round_weight("w1_bf1", w1_a1, first, on_vector)
+        magnitude(0)
+        project_keyword(1, quantize("w1_q1", w1_bf1), first)
+        empty(1, on_scalar)
+        w2_q = quantize("w2_q2", round_weight("w2_bf2", w2_hi, both, on_vector))
+        look_up(0)
+        project_synonym(2, w2_q, first)
+        project_synonym(3, w2_q, second)
+        w1_q = quantize("w1_q2", round_weight("w1_bf2", w1_hi, both, on_vector))
+        magnitude(1)
+        project_keyword(2, w1_q, first)
+        bst = best(0, every, "w1_bf2")
+        project_keyword(3, w1_q, second)
+        look_up(1)
+        empty(2, on_vector)
+        weigh(0, every, bst, nc.vector)
+        empty(3, on_vector)
+        magnitude(2)
+        bst = best(1, every, "bst1")
+        es_pick = gather_scales("es_pick", es_table, adk_t[:], "w1_bf2")
+        weigh(1, every, bst, nc.vector)
+        look_up(2)
+        magnitude(3)
+        look_up(3)
+        weigh(2, every, best(2, every, "bst2"), nc.vector)
+        bst = [best(3, halves[h], f"bst3{h}") for h in range(2)]
+        for h in range(2):
+            weigh(3, halves[h], bst[h], nc.vector)
+        e_pick = (gather_words("e_pick", e_table, adk_t[:], "bst31"), es_pick)
+        for n in range(3):
+            rs[n] = inverse_root(f"{n}", square(f"{n}", dealt[n]))
+        for n in range(3):
+            saturate(n)
+        sat_t = [turn_back(h, sat) for h in range(2)]
+        strict = sb.tile([P, Z], F32, name="strict", tag="sq2")
         nc.scalar.activation(strict[:], mth_t[:].indirect(adk_t[:]), ACT.Copy)
-        rs1.append(inverse_norm("1b", q1[1][:], "sq1b"))
-        excl0 = exclude(0, sc0)
-        sat1 = sb.tile([P, PACK, P], F32, name="sat1")
-        for r in range(2):
-            saturate(sat1[:, :, r * P // 2 : (r + 1) * P // 2], q1[r][:], rs1[r])
-        hid1 = hidden(1, turn_back(1, sat1))
-        sc1 = score(1, hid1)
-        finish(0, excl0)
-        finish(1, exclude(1, sc1))
+        hid = [hidden(h, sat_t[h]) for h in range(2)]
+        sc = [score(h, hid[h]) for h in range(2)]
+        excl = [exclude(h, sc[h]) for h in range(2)]
+        broad = [broader(h, excl[h]) for h in range(2)]
+        xm = [scaled(0, excl[0], nc.vector), scaled(1, excl[1], nc.vector)]
+        finish(0, xm[0], broad[0], [every])
+        finish(1, xm[1], broad[1], halves)

@@ -15,41 +15,54 @@ ACT = mybir.ActivationFunctionType
 
 P = 128
 PACK = 4
-K, T, S, H, Z = 512, 2048, 512, 512, 512
-V = S // 2
-HALF = S // 2
-FLOPS = 2 * (2 * K * H * S + H * V * Z)
+K = 512
+H = 512
+TABLE = 2048
+LIST = 512
+HALF = LIST // 2
+HALF_COLS = HALF // 16
+PAIR = 2
+GROUP = 4
+Y_BANKS = 3
+TILE_SETS = ((0, 1), (2,), (3,))
+FLOPS = 2 * (2 * K * H * LIST + H * (LIST // PAIR) * LIST)
 
 
 def tile_picked_ysponsq_min_p_kernel(
     tc, x_words, x_scales, w1, w2, e_words, e_scales, unit, mth, offs, syn, adk, brd, out
 ):
     nc = tc.nc
+    on_vector, on_scalar = nc.vector.tensor_copy, nc.scalar.copy
+    first, second, both = slice(0, P), slice(P, 2 * P), slice(0, 2 * P)
+    every = slice(0, LIST)
+    halves = [slice(h * HALF, (h + 1) * HALF) for h in range(2)]
+    list_halves = [slice(h * HALF_COLS, (h + 1) * HALF_COLS) for h in range(2)]
+
     with ExitStack() as ctx:
         sb = ctx.enter_context(tc.tile_pool(name="sb", bufs=1))
         ps = ctx.enter_context(tc.psum_pool(name="ps", bufs=1))
 
         def load_list(name, src):
-            lst = sb.tile([P, S // 16], U16, name=name)
+            lst = sb.tile([P, LIST // 16], U16, name=name)
             nc.sync.dma_start(lst[:], src)
             return lst
 
         def load_words(name, src):
-            words = sb.tile([P, T], I32, name=name)
+            words = sb.tile([P, TABLE], I32, name=name)
             nc.sync.dma_start(words[:], src[0].rearrange("p n t -> p (n t)").bitcast(I32))
             return words
 
-        def load_scales(name, src, clear, queue):
-            plane = sb.tile([P, T], U8, name=name)
-            clear.memset(plane[:].bitcast(I32), 0)
-            rows = src[0].bitcast(I32)
+        def load_scales(name, src, clear):
+            rows = sb.tile([P, TABLE], U8, name=name, tag=name, align_bytes=64)
+            clear.memset(rows[:].bitcast(I32), 0)
+            src_rows = src[0].bitcast(I32)
             for r in range(4):
-                queue.dma_start(plane[r:P:32, :].bitcast(I32), rows[r:16:4, :])
-            return plane
+                nc.sync.dma_start(rows[r:P:32, :].bitcast(I32), src_rows[r:16:4, :])
+            return rows
 
-        def load_weight(name, src, lo, hi):
-            raw = sb.tile([P, PACK, hi - lo], F32, name=name)
-            nc.sync.dma_start(raw[:], src.rearrange("(p j) c -> p j c", j=PACK)[:, :, lo:hi])
+        def load_weight(name, src, lo):
+            raw = sb.tile([P, PACK, 2 * P], F32, name=name)
+            nc.sync.dma_start(raw[:], src.rearrange("(p j) c -> p j c", j=PACK)[:, :, lo : lo + 2 * P])
             return raw
 
         def gather_words(name, table, lst, tag):
@@ -58,22 +71,22 @@ def tile_picked_ysponsq_min_p_kernel(
             return picked[:]
 
         def gather_scales(name, table, lst, tag):
-            picked = sb.tile([P, S], U8, name=name, tag=tag, align_bytes=64)
+            picked = sb.tile([P, LIST], U8, name=name, tag=tag, align_bytes=64)
             nc.vector.tensor_copy(picked[:], table[:].indirect(lst))
             return picked[:]
 
-        def round_weight(name, raw, cols, copy, tag=None):
+        def round_weight(name, raw, cols, copy):
             part = raw[:, :, cols]
-            grouped = sb.tile([P, part.shape[2], PACK], BF16, name=name, tag=tag or name, align_bytes=64)
+            grouped = sb.tile([P, part.shape[2], PACK], BF16, name=name, tag=name, align_bytes=64)
             copy(
                 grouped[:].rearrange("p (c i) j -> p c j i", i=4),
                 part.rearrange("p j (c i) -> p c j i", i=4),
             )
             return grouped
 
-        def quantize(name, grouped):
+        def quantize(name, grouped, tag=None):
             width = grouped.shape[1]
-            codes = sb.tile([P, width], U32, name=name + "_codes", align_bytes=64)
+            codes = sb.tile([P, width], U32, name=name + "_codes", tag=tag or name, align_bytes=64)
             scales = sb.tile([P, width], U8, name=name + "_scales", align_bytes=64)
             nc.vector.quantize_mx(
                 out=codes[:].bitcast(FP8X4),
@@ -97,89 +110,100 @@ def tile_picked_ysponsq_min_p_kernel(
         nc.vector.memset(warm[:], 1.0)
         warm_out = sb.tile([P, 1], F32, name="warm_out")
         nc.scalar.activation(warm_out[:], warm[:], ACT.Abs_reciprocal_sqrt)
+
         offs_t = load_list("offs_t", offs)
-        w2_a0 = load_weight("w2_a0", w2, 0, P)
-        xs_table = load_scales("xs_table", x_scales, nc.gpsimd, nc.sync)
+        w2_lo = load_weight("w2_lo", w2, 0)
+        xs_table = load_scales("xs_table", x_scales, nc.gpsimd)
         x_table = load_words("x_table", x_words)
         ident = sb.tile([P, P], F32, name="ident")
         make_identity(nc, ident[:])
-        w1_a0 = load_weight("w1_a0", w1, 0, P)
+        w1_lo = load_weight("w1_lo", w1, 0)
         syn_t = load_list("syn_t", syn)
-        w2_a1 = load_weight("w2_a1", w2, P, 2 * P)
-        w1_a1 = load_weight("w1_a1", w1, P, 2 * P)
-        w2_hi = load_weight("w2_hi", w2, 2 * P, H)
-        w1_hi = load_weight("w1_hi", w1, 2 * P, H)
+        w2_hi = load_weight("w2_hi", w2, 2 * P)
+        w1_hi = load_weight("w1_hi", w1, 2 * P)
         adk_t = load_list("adk_t", adk)
-        es_table = load_scales("es_table", e_scales, nc.vector, nc.sync)
+        es_table = load_scales("es_table", e_scales, nc.vector)
         e_table = load_words("e_table", e_words)
         unit_t = sb.tile([P, PACK], F32, name="unit_t")
         nc.sync.dma_start(unit_t[:], unit.rearrange("(p t) o -> p (t o)", t=PACK))
         brd_t = load_list("brd_t", brd)
-        mth_t = sb.tile([P, T], F32, name="mth_t")
+        mth_t = sb.tile([P, TABLE], F32, name="mth_t")
         nc.sync.dma_start(mth_t[:], mth)
 
-        first, second, both = slice(0, P), slice(P, 2 * P), slice(0, 2 * P)
-        y_ps, yg_ps, yg_sb, mag, gs, bst = {}, {}, {}, {}, {}, {}
-        halves = [slice(h * HALF, (h + 1) * HALF) for h in range(2)]
+        y_ps, yg_ps, yg_sb, mag, gs, rs = {}, {}, {}, {}, {}, {}
+
+        def paired(cols):
+            return cols.rearrange("p (h v d) -> p h d v", v=P, d=PAIR)
+
+        def split(cols):
+            return cols.rearrange("p (h d v) -> p h d v", v=P, d=PAIR)
 
         def project(acc, w_q, rows):
             for h in range(2):
                 product(acc[:, halves[h]], w_q, rows, x_pick[h], both)
 
         def project_synonym(a, w_q, rows):
-            yg_ps[a] = ps.tile([P, S], F32, name=f"yg_ps{a}", tag="turn", bufs=2)
+            yg_ps[a] = ps.tile([P, LIST], F32, name=f"yg_ps{a}", tag="turn", bufs=2)
             project(yg_ps[a], w_q, rows)
 
         def project_keyword(a, w_q, rows):
-            y_ps[a] = ps.tile([P, S], F32, name=f"y_ps{a}", tag="y_bank", bufs=3)
+            y_ps[a] = ps.tile([P, LIST], F32, name=f"y_ps{a}", tag="y_bank", bufs=Y_BANKS)
             project(y_ps[a], w_q, rows)
 
         def empty(a, copy):
-            yg_sb[a] = sb.tile([P, S], F32, name=f"yg_sb{a}")
+            yg_sb[a] = sb.tile([P, LIST], F32, name=f"yg_sb{a}")
             copy(yg_sb[a][:], yg_ps[a][:])
 
         def magnitude(a):
-            mag[a] = sb.tile([P, S], F32, name=f"mag{a}")
-            nc.scalar.activation(mag[a][:], y_ps[a][:], ACT.Abs)
+            mag[a] = sb.tile([P, LIST], F32, name=f"mag{a}")
+            nc.scalar.activation(split(mag[a][:]), paired(y_ps[a][:]), ACT.Abs)
 
         def look_up(a):
-            gs[a] = sb.tile([P, S], F32, name=f"gs{a}")
+            gs[a] = sb.tile([P, LIST], F32, name=f"gs{a}", tag=f"gs{a}", align_bytes=64)
             for h in range(2):
-                window = yg_sb[a][:].indirect(syn_t[:, h * 16 : (h + 1) * 16])
+                window = yg_sb[a][:].indirect(syn_t[:, list_halves[h]])
                 nc.scalar.activation(gs[a][:, halves[h]], window, ACT.Copy)
 
-        def best(a, cols, tag):
-            bst = sb.tile([P, cols.stop - cols.start], F32, name=f"bst{a}_{cols.start}", tag=tag, align_bytes=64)
-            nc.vector.tensor_tensor(bst[:], y_ps[a][:, cols], gs[a][:, cols], ALU.max)
+        def best(a, parts, tag):
+            bst = sb.tile([P, LIST], F32, name=f"bst{a}", tag=tag, align_bytes=64)
+            for cols in parts:
+                nc.vector.tensor_tensor(
+                    split(bst[:, cols]), paired(y_ps[a][:, cols]), paired(gs[a][:, cols]), ALU.max
+                )
             return bst
 
-        def weigh(a, cols, bst, engine):
+        def weigh(a, cols, bst):
             aw = sb.tile([P, cols.stop - cols.start], F32, name=f"aw{a}_{cols.start}")
-            engine.tensor_tensor(aw[:], bst[:], mag[a][:, cols], ALU.mult)
-            n = max(a - 1, 0)
-            col = (a - groups[n][0]) * P
+            nc.vector.tensor_tensor(aw[:], bst[:, cols], mag[a][:, cols], ALU.mult)
+            n = [a in tiles for tiles in TILE_SETS].index(True)
+            col = (a - TILE_SETS[n][0]) * P
             for lo in range(0, cols.stop - cols.start, HALF):
-                for d in range(2):
+                for d in range(PAIR):
                     nc.tensor.matmul(
                         q_bank[n][:, (cols.start + lo) // HALF, col : col + P],
-                        aw[:, lo + d : lo + HALF : 2],
+                        aw[:, lo + d * P : lo + (d + 1) * P],
                         ident[:],
                         start=(d == 0),
-                        stop=(d == 1),
+                        stop=(d == PAIR - 1),
                         is_transpose=True,
                     )
 
-        def square(name, dealt):
-            sq = sb.tile(list(dealt.shape), F32, name="sq" + name, tag="sq" + name)
-            nc.scalar.activation(sq[:], dealt, ACT.Square)
-            return sq
+        def best_and_weigh_by_halves(a, tag):
+            bst = best(a, halves, tag)
+            for cols in halves:
+                weigh(a, cols, bst)
 
-        def inverse_root(name, sq):
-            rs = sb.tile(list(sq.shape), F32, name="rs" + name, tag="rs" + name, align_bytes=64)
-            nc.scalar.activation(rs[:], sq[:], ACT.Abs_reciprocal_sqrt, bias=0.5)
-            return rs
+        def inverse_norm(n):
+            sq = sb.tile(list(dealt[n].shape), F32, name=f"sq{n}", tag=f"sq{n}")
+            nc.scalar.activation(sq[:], dealt[n], ACT.Square)
+            rs[n] = sb.tile(list(sq.shape), F32, name=f"rs{n}", tag=f"rs{n}", align_bytes=64)
+            nc.scalar.activation(rs[n][:], sq[:], ACT.Abs_reciprocal_sqrt, bias=0.5)
 
-        def turn_back(h, sat):
+        def saturate(n):
+            lo, hi = TILE_SETS[n][0] * P // PACK, (TILE_SETS[n][-1] + 1) * P // PACK
+            nc.vector.tensor_tensor(sat[:, :, :, lo:hi], dealt[n], rs[n][:], ALU.mult)
+
+        def turn_back(h):
             sat_t = ps.tile([P, PACK, P], F32, name=f"sat_t{h}", tag="turn", bufs=2)
             for t in range(PACK):
                 nc.tensor.transpose(sat_t[:, t, :], sat[:, h, t, :], ident[:])
@@ -199,37 +223,37 @@ def tile_picked_ysponsq_min_p_kernel(
             hid_q = quantize(f"hid_q{h}", hid)
             sc = []
             for c in range(2):
-                sc.append(ps.tile([P, Z // 2], F32, name=f"sc{h}{c}", tag=("y_bank", "y_bank", "y_bank", "q_bank0")[2 * h + c], bufs=(3, 3, 3, 1)[2 * h + c]))
-                product(sc[c][:], hid_q, first, e_pick, slice(c * Z // 2, (c + 1) * Z // 2))
+                tag, bufs = ("y_bank", Y_BANKS) if 2 * h + c < Y_BANKS else ("q_bank0", 1)
+                sc.append(ps.tile([P, HALF], F32, name=f"sc{h}{c}", tag=tag, bufs=bufs))
+                product(sc[c][:], hid_q, first, e_pick, halves[c])
             return sc
 
         def exclude(h, sc):
-            total = sb.tile([P, 2, Z // 8], F32, name=f"total{h}")
-            excl = sb.tile([P, Z], F32, name=f"excl{h}")
-            groups = [sc[c][:].rearrange("v (z d) -> v z d", d=4) for c in range(2)]
+            total = sb.tile([P, 2, HALF // GROUP], F32, name=f"total{h}")
+            excl = sb.tile([P, LIST], F32, name=f"excl{h}")
+            grouped = [sc[c][:].rearrange("v (z d) -> v z d", d=GROUP) for c in range(2)]
             for c in range(2):
-                nc.vector.tensor_reduce(total[:, c, :], groups[c], mybir.AxisListType.X, ALU.add)
+                nc.vector.tensor_reduce(total[:, c, :], grouped[c], mybir.AxisListType.X, ALU.add)
             for c in range(2):
                 nc.vector.scalar_tensor_tensor(
-                    excl[:, c * Z // 2 : (c + 1) * Z // 2].rearrange("v (z d) -> v z d", d=4),
-                    total[:, c, :].unsqueeze(2).to_broadcast([P, Z // 8, 4]),
-                    -0.8 / 4,
-                    groups[c],
+                    excl[:, halves[c]].rearrange("v (z d) -> v z d", d=GROUP),
+                    total[:, c, :].unsqueeze(2).to_broadcast([P, HALF // GROUP, GROUP]),
+                    -0.8 / GROUP,
+                    grouped[c],
                     ALU.mult,
                     ALU.add,
                 )
             return excl
 
         def broader(h, excl):
-            broad = sb.tile([P, Z], F32, name=f"broad{h}")
+            broad = sb.tile([P, LIST], F32, name=f"broad{h}")
             for c in range(2):
-                nc.scalar.activation(
-                    broad[:, halves[c]], excl[:].indirect(brd_t[:, c * 16 : (c + 1) * 16]), ACT.Copy
-                )
+                window = excl[:].indirect(brd_t[:, list_halves[c]])
+                nc.scalar.activation(broad[:, halves[c]], window, ACT.Copy)
             return broad
 
         def scaled(h, excl, engine):
-            xm = sb.tile([P, Z], F32, name=f"xm{h}")
+            xm = sb.tile([P, LIST], F32, name=f"xm{h}")
             engine.tensor_tensor(xm[:], excl[:], strict[:], ALU.mult)
             return xm
 
@@ -239,71 +263,65 @@ def tile_picked_ysponsq_min_p_kernel(
                 nc.vector.tensor_tensor(res[:], xm[:, cols], broad[:, cols], ALU.min)
                 nc.sync.dma_start(out[h * P : (h + 1) * P, cols], res[:])
 
-        on_vector, on_scalar = nc.vector.tensor_copy, nc.scalar.copy
-        w2_bf = [round_weight("w2_bf0", w2_a0, first, on_scalar)]
+        w2_bf0 = round_weight("w2_bf0", w2_lo, both, on_scalar)
         xs_pick = gather_scales("xs_pick", xs_table, offs_t[:], "xs_pick")
-        w2_q0 = quantize("w2_q0", w2_bf[0])
+        w2_q0 = quantize("w2_q0", w2_bf0, "xs_table")
         x_pick = [
-            (gather_words(f"x_pick{h}", x_table, offs_t[:, h * 16 : (h + 1) * 16], f"x_pick{h}"), xs_pick[:, h * HALF : (h + 1) * HALF])
+            (gather_words(f"x_pick{h}", x_table, offs_t[:, list_halves[h]], f"x_pick{h}"), xs_pick[:, halves[h]])
             for h in range(2)
         ]
-        every = slice(0, S)
-        groups = ((0, 1), (2,), (3,))
-        q_bank = [ps.tile([P, 2, len(g) * P], F32, name=f"q_bank{n}", tag=f"q_bank{n}") for n, g in enumerate(groups)]
+
+        q_bank = [
+            ps.tile([P, 2, len(tiles) * P], F32, name=f"q_bank{n}", tag=f"q_bank{n}")
+            for n, tiles in enumerate(TILE_SETS)
+        ]
         dealt = [q[:].rearrange("v h (p t) -> v h t p", t=PACK) for q in q_bank]
-        rs = {}
-
-        def saturate(n):
-            lo, hi = groups[n][0] * P // PACK, (groups[n][-1] + 1) * P // PACK
-            nc.vector.tensor_tensor(sat[:, :, :, lo:hi], dealt[n], rs[n][:], ALU.mult)
-
         sat = sb.tile([P, 2, PACK, P], F32, name="sat")
+
         project_synonym(0, w2_q0, first)
-        w1_bf0 = round_weight("w1_bf0", w1_a0, first, on_scalar)
+        project_synonym(1, w2_q0, second)
+        w1_bf0 = round_weight("w1_bf0", w1_lo, first, on_vector)
         empty(0, on_scalar)
-        w2_bf1 = round_weight("w2_bf1", w2_a1, first, on_vector)
         project_keyword(0, quantize("w1_q0", w1_bf0), first)
-        project_synonym(1, quantize("w2_q1", w2_bf1), first)
-        w1_bf1 = round_weight("w1_bf1", w1_a1, first, on_vector)
+        w1_bf1 = round_weight("w1_bf1", w1_lo, second, on_vector)
         magnitude(0)
         project_keyword(1, quantize("w1_q1", w1_bf1), first)
         empty(1, on_scalar)
-        w2_q = quantize("w2_q2", round_weight("w2_bf2", w2_hi, both, on_vector))
+        w2_q2 = quantize("w2_q2", round_weight("w2_bf2", w2_hi, both, on_vector))
         look_up(0)
-        project_synonym(2, w2_q, first)
-        project_synonym(3, w2_q, second)
-        w1_q = quantize("w1_q2", round_weight("w1_bf2", w1_hi, both, on_vector))
+        project_synonym(2, w2_q2, first)
+        project_synonym(3, w2_q2, second)
+        w1_q2 = quantize("w1_q2", round_weight("w1_bf2", w1_hi, both, on_vector))
         magnitude(1)
-        project_keyword(2, w1_q, first)
-        bst = best(0, every, "w1_bf2")
-        project_keyword(3, w1_q, second)
+        project_keyword(2, w1_q2, first)
+        bst0 = best(0, [every], "w1_bf2")
+        project_keyword(3, w1_q2, second)
         look_up(1)
         empty(2, on_vector)
-        weigh(0, every, bst, nc.vector)
+        weigh(0, every, bst0)
         empty(3, on_vector)
         magnitude(2)
-        bst = best(1, every, "bst1")
-        es_pick = gather_scales("es_pick", es_table, adk_t[:], "w1_bf2")
-        weigh(1, every, bst, nc.vector)
+        best_and_weigh_by_halves(1, "gs0")
         look_up(2)
         magnitude(3)
         look_up(3)
-        weigh(2, every, best(2, every, "bst2"), nc.vector)
-        bst = [best(3, halves[h], f"bst3{h}") for h in range(2)]
-        for h in range(2):
-            weigh(3, halves[h], bst[h], nc.vector)
-        e_pick = (gather_words("e_pick", e_table, adk_t[:], "bst31"), es_pick)
-        for n in range(3):
-            rs[n] = inverse_root(f"{n}", square(f"{n}", dealt[n]))
-        for n in range(3):
+        best_and_weigh_by_halves(2, "gs1")
+        best_and_weigh_by_halves(3, "gs2")
+
+        e_words_pick = gather_words("e_pick", e_table, adk_t[:], "gs3")
+        for n in range(len(TILE_SETS)):
+            inverse_norm(n)
+        for n in range(len(TILE_SETS)):
             saturate(n)
-        sat_t = [turn_back(h, sat) for h in range(2)]
-        strict = sb.tile([P, Z], F32, name="strict", tag="sq2")
+        sat_t = [turn_back(h) for h in range(2)]
+        e_pick = (e_words_pick, gather_scales("es_pick", es_table, adk_t[:], "rs2"))
+        strict = sb.tile([P, LIST], F32, name="strict", tag="sq2")
         nc.scalar.activation(strict[:], mth_t[:].indirect(adk_t[:]), ACT.Copy)
+
         hid = [hidden(h, sat_t[h]) for h in range(2)]
         sc = [score(h, hid[h]) for h in range(2)]
         excl = [exclude(h, sc[h]) for h in range(2)]
         broad = [broader(h, excl[h]) for h in range(2)]
         xm = [scaled(0, excl[0], nc.vector), scaled(1, excl[1], nc.vector)]
-        finish(0, xm[0], broad[0], [every])
+        finish(0, xm[0], broad[0], halves)
         finish(1, xm[1], broad[1], halves)

from contextlib import ExitStack

import concourse.mybir as mybir
from concourse.masks import make_identity

F32 = mybir.dt.float32
BF16 = mybir.dt.bfloat16
I32 = mybir.dt.int32
U32 = mybir.dt.uint32
U16 = mybir.dt.uint16
U8 = mybir.dt.uint8
FP8X4 = mybir.dt.float8_e4m3fn_x4
ALU = mybir.AluOpType
ACT = mybir.ActivationFunctionType

P = 128
PACK = 4
K = 512
H = 512
TABLE = 2048
LIST = 512
HALF = LIST // 2
HALF_COLS = HALF // 16
PAIR = 2
GROUP = 4
Y_BANKS = 3
TILE_SETS = ((0, 1), (2,), (3,))
FLOPS = 2 * (2 * K * H * LIST + H * (LIST // PAIR) * LIST)


def tile_picked_ysponsq_min_p_kernel(
    tc, x_words, x_scales, w1, w2, e_words, e_scales, unit, mth, offs, syn, adk, brd, out
):
    nc = tc.nc
    on_vector, on_scalar = nc.vector.tensor_copy, nc.scalar.copy
    first, second, both = slice(0, P), slice(P, 2 * P), slice(0, 2 * P)
    every = slice(0, LIST)
    halves = [slice(h * HALF, (h + 1) * HALF) for h in range(2)]
    list_halves = [slice(h * HALF_COLS, (h + 1) * HALF_COLS) for h in range(2)]

    with ExitStack() as ctx:
        sb = ctx.enter_context(tc.tile_pool(name="sb", bufs=1))
        ps = ctx.enter_context(tc.psum_pool(name="ps", bufs=1))

        def load_list(name, src):
            lst = sb.tile([P, LIST // 16], U16, name=name)
            nc.sync.dma_start(lst[:], src)
            return lst

        def load_words(name, src):
            words = sb.tile([P, TABLE], I32, name=name)
            nc.sync.dma_start(words[:], src[0].rearrange("p n t -> p (n t)").bitcast(I32))
            return words

        def load_scales(name, src, clear):
            rows = sb.tile([P, TABLE], U8, name=name, tag=name, align_bytes=64)
            clear.memset(rows[:].bitcast(I32), 0)
            src_rows = src[0].bitcast(I32)
            for r in range(4):
                nc.sync.dma_start(rows[r:P:32, :].bitcast(I32), src_rows[r:16:4, :])
            return rows

        def load_weight(name, src, lo):
            raw = sb.tile([P, PACK, 2 * P], F32, name=name)
            nc.sync.dma_start(raw[:], src.rearrange("(p j) c -> p j c", j=PACK)[:, :, lo : lo + 2 * P])
            return raw

        def gather_words(name, table, lst, tag):
            picked = sb.tile([P, lst.shape[1] * 16], U32, name=name, tag=tag, align_bytes=64)
            nc.vector.tensor_copy(picked[:], table[:].bitcast(U32).indirect(lst))
            return picked[:]

        def gather_scales(name, table, lst, tag):
            picked = sb.tile([P, LIST], U8, name=name, tag=tag, align_bytes=64)
            nc.vector.tensor_copy(picked[:], table[:].indirect(lst))
            return picked[:]

        def round_weight(name, raw, cols, copy):
            part = raw[:, :, cols]
            grouped = sb.tile([P, part.shape[2], PACK], BF16, name=name, tag=name, align_bytes=64)
            copy(
                grouped[:].rearrange("p (c i) j -> p c j i", i=4),
                part.rearrange("p j (c i) -> p c j i", i=4),
            )
            return grouped

        def quantize(name, grouped, tag=None):
            width = grouped.shape[1]
            codes = sb.tile([P, width], U32, name=name + "_codes", tag=tag or name, align_bytes=64)
            scales = sb.tile([P, width], U8, name=name + "_scales", align_bytes=64)
            nc.vector.quantize_mx(
                out=codes[:].bitcast(FP8X4),
                scales=scales[:],
                in_=grouped[:].rearrange("p c j -> p (c j)"),
            )
            return codes, scales

        def product(acc, stationary, rows, moving, cols):
            nc.tensor.matmul_mx(
                out=acc,
                lhsT=stationary[0][:, rows].bitcast(FP8X4),
                lhsT_scale=stationary[1][:, rows],
                rhs=moving[0][:, cols].bitcast(FP8X4),
                rhs_scale=moving[1][:, cols],
                start=True,
                stop=True,
            )

        warm = sb.tile([P, 1], F32, name="warm")
        nc.vector.memset(warm[:], 1.0)
        warm_out = sb.tile([P, 1], F32, name="warm_out")
        nc.scalar.activation(warm_out[:], warm[:], ACT.Abs_reciprocal_sqrt)

        offs_t = load_list("offs_t", offs)
        w2_lo = load_weight("w2_lo", w2, 0)
        xs_table = load_scales("xs_table", x_scales, nc.gpsimd)
        x_table = load_words("x_table", x_words)
        ident = sb.tile([P, P], F32, name="ident")
        make_identity(nc, ident[:])
        w1_lo = load_weight("w1_lo", w1, 0)
        syn_t = load_list("syn_t", syn)
        w2_hi = load_weight("w2_hi", w2, 2 * P)
        w1_hi = load_weight("w1_hi", w1, 2 * P)
        adk_t = load_list("adk_t", adk)
        es_table = load_scales("es_table", e_scales, nc.vector)
        e_table = load_words("e_table", e_words)
        unit_t = sb.tile([P, PACK], F32, name="unit_t")
        nc.sync.dma_start(unit_t[:], unit.rearrange("(p t) o -> p (t o)", t=PACK))
        brd_t = load_list("brd_t", brd)
        mth_t = sb.tile([P, TABLE], F32, name="mth_t")
        nc.sync.dma_start(mth_t[:], mth)

        y_ps, yg_ps, yg_sb, mag, gs, rs = {}, {}, {}, {}, {}, {}

        def paired(cols):
            return cols.rearrange("p (h v d) -> p h d v", v=P, d=PAIR)

        def split(cols):
            return cols.rearrange("p (h d v) -> p h d v", v=P, d=PAIR)

        def project(acc, w_q, rows):
            for h in range(2):
                product(acc[:, halves[h]], w_q, rows, x_pick[h], both)

        def project_synonym(a, w_q, rows):
            yg_ps[a] = ps.tile([P, LIST], F32, name=f"yg_ps{a}", tag="turn", bufs=2)
            project(yg_ps[a], w_q, rows)

        def project_keyword(a, w_q, rows):
            y_ps[a] = ps.tile([P, LIST], F32, name=f"y_ps{a}", tag="y_bank", bufs=Y_BANKS)
            project(y_ps[a], w_q, rows)

        def empty(a, copy):
            yg_sb[a] = sb.tile([P, LIST], F32, name=f"yg_sb{a}")
            copy(yg_sb[a][:], yg_ps[a][:])

        def magnitude(a):
            mag[a] = sb.tile([P, LIST], F32, name=f"mag{a}")
            nc.scalar.activation(split(mag[a][:]), paired(y_ps[a][:]), ACT.Abs)

        def look_up(a):
            gs[a] = sb.tile([P, LIST], F32, name=f"gs{a}", tag=f"gs{a}", align_bytes=64)
            for h in range(2):
                window = yg_sb[a][:].indirect(syn_t[:, list_halves[h]])
                nc.scalar.activation(gs[a][:, halves[h]], window, ACT.Copy)

        def best(a, parts, tag):
            bst = sb.tile([P, LIST], F32, name=f"bst{a}", tag=tag, align_bytes=64)
            for cols in parts:
                nc.vector.tensor_tensor(
                    split(bst[:, cols]), paired(y_ps[a][:, cols]), paired(gs[a][:, cols]), ALU.max
                )
            return bst

        def weigh(a, cols, bst):
            aw = sb.tile([P, cols.stop - cols.start], F32, name=f"aw{a}_{cols.start}")
            nc.vector.tensor_tensor(aw[:], bst[:, cols], mag[a][:, cols], ALU.mult)
            n = [a in tiles for tiles in TILE_SETS].index(True)
            col = (a - TILE_SETS[n][0]) * P
            for lo in range(0, cols.stop - cols.start, HALF):
                for d in range(PAIR):
                    nc.tensor.matmul(
                        q_bank[n][:, (cols.start + lo) // HALF, col : col + P],
                        aw[:, lo + d * P : lo + (d + 1) * P],
                        ident[:],
                        start=(d == 0),
                        stop=(d == PAIR - 1),
                        is_transpose=True,
                    )

        def best_and_weigh_by_halves(a, tag):
            bst = best(a, halves, tag)
            for cols in halves:
                weigh(a, cols, bst)

        def inverse_norm(n):
            sq = sb.tile(list(dealt[n].shape), F32, name=f"sq{n}", tag=f"sq{n}")
            nc.scalar.activation(sq[:], dealt[n], ACT.Square)
            rs[n] = sb.tile(list(sq.shape), F32, name=f"rs{n}", tag=f"rs{n}", align_bytes=64)
            nc.scalar.activation(rs[n][:], sq[:], ACT.Abs_reciprocal_sqrt, bias=0.5)

        def saturate(n):
            lo, hi = TILE_SETS[n][0] * P // PACK, (TILE_SETS[n][-1] + 1) * P // PACK
            nc.vector.tensor_tensor(sat[:, :, :, lo:hi], dealt[n], rs[n][:], ALU.mult)

        def turn_back(h):
            sat_t = ps.tile([P, PACK, P], F32, name=f"sat_t{h}", tag="turn", bufs=2)
            for t in range(PACK):
                nc.tensor.transpose(sat_t[:, t, :], sat[:, h, t, :], ident[:])
            return sat_t

        def hidden(h, sat_t):
            hid = sb.tile([P, P, PACK], BF16, name=f"hid{h}", align_bytes=64)
            nc.vector.tensor_tensor(
                hid[:],
                sat_t[:].rearrange("p t v -> p v t"),
                unit_t[:].unsqueeze(1).to_broadcast([P, P, PACK]),
                ALU.mult,
            )
            return hid

        def score(h, hid):
            hid_q = quantize(f"hid_q{h}", hid)
            sc = []
            for c in range(2):
                tag, bufs = ("y_bank", Y_BANKS) if 2 * h + c < Y_BANKS else ("q_bank0", 1)
                sc.append(ps.tile([P, HALF], F32, name=f"sc{h}{c}", tag=tag, bufs=bufs))
                product(sc[c][:], hid_q, first, e_pick, halves[c])
            return sc

        def exclude(h, sc):
            total = sb.tile([P, 2, HALF // GROUP], F32, name=f"total{h}")
            excl = sb.tile([P, LIST], F32, name=f"excl{h}")
            grouped = [sc[c][:].rearrange("v (z d) -> v z d", d=GROUP) for c in range(2)]
            for c in range(2):
                nc.vector.tensor_reduce(total[:, c, :], grouped[c], mybir.AxisListType.X, ALU.add)
            for c in range(2):
                nc.vector.scalar_tensor_tensor(
                    excl[:, halves[c]].rearrange("v (z d) -> v z d", d=GROUP),
                    total[:, c, :].unsqueeze(2).to_broadcast([P, HALF // GROUP, GROUP]),
                    -0.8 / GROUP,
                    grouped[c],
                    ALU.mult,
                    ALU.add,
                )
            return excl

        def broader(h, excl):
            broad = sb.tile([P, LIST], F32, name=f"broad{h}")
            for c in range(2):
                window = excl[:].indirect(brd_t[:, list_halves[c]])
                nc.scalar.activation(broad[:, halves[c]], window, ACT.Copy)
            return broad

        def scaled(h, excl, engine):
            xm = sb.tile([P, LIST], F32, name=f"xm{h}")
            engine.tensor_tensor(xm[:], excl[:], strict[:], ALU.mult)
            return xm

        def finish(h, xm, broad, parts):
            for n, cols in enumerate(parts):
                res = sb.tile([P, cols.stop - cols.start], F32, name=f"res{h}{n}")
                nc.vector.tensor_tensor(res[:], xm[:, cols], broad[:, cols], ALU.min)
                nc.sync.dma_start(out[h * P : (h + 1) * P, cols], res[:])

        w2_bf0 = round_weight("w2_bf0", w2_lo, both, on_scalar)
        xs_pick = gather_scales("xs_pick", xs_table, offs_t[:], "xs_pick")
        w2_q0 = quantize("w2_q0", w2_bf0, "xs_table")
        x_pick = [
            (gather_words(f"x_pick{h}", x_table, offs_t[:, list_halves[h]], f"x_pick{h}"), xs_pick[:, halves[h]])
            for h in range(2)
        ]

        q_bank = [
            ps.tile([P, 2, len(tiles) * P], F32, name=f"q_bank{n}", tag=f"q_bank{n}")
            for n, tiles in enumerate(TILE_SETS)
        ]
        dealt = [q[:].rearrange("v h (p t) -> v h t p", t=PACK) for q in q_bank]
        sat = sb.tile([P, 2, PACK, P], F32, name="sat")

        project_synonym(0, w2_q0, first)
        project_synonym(1, w2_q0, second)
        w1_bf0 = round_weight("w1_bf0", w1_lo, first, on_vector)
        empty(0, on_scalar)
        project_keyword(0, quantize("w1_q0", w1_bf0), first)
        w1_bf1 = round_weight("w1_bf1", w1_lo, second, on_vector)
        magnitude(0)
        project_keyword(1, quantize("w1_q1", w1_bf1), first)
        empty(1, on_scalar)
        w2_q2 = quantize("w2_q2", round_weight("w2_bf2", w2_hi, both, on_vector))
        look_up(0)
        project_synonym(2, w2_q2, first)
        project_synonym(3, w2_q2, second)
        w1_q2 = quantize("w1_q2", round_weight("w1_bf2", w1_hi, both, on_vector))
        magnitude(1)
        project_keyword(2, w1_q2, first)
        bst0 = best(0, [every], "w1_bf2")
        project_keyword(3, w1_q2, second)
        look_up(1)
        empty(2, on_vector)
        weigh(0, every, bst0)
        empty(3, on_vector)
        magnitude(2)
        best_and_weigh_by_halves(1, "gs0")
        look_up(2)
        magnitude(3)
        look_up(3)
        best_and_weigh_by_halves(2, "gs1")
        best_and_weigh_by_halves(3, "gs2")

        e_words_pick = gather_words("e_pick", e_table, adk_t[:], "gs3")
        for n in range(len(TILE_SETS)):
            inverse_norm(n)
        for n in range(len(TILE_SETS)):
            saturate(n)
        sat_t = [turn_back(h) for h in range(2)]
        e_pick = (e_words_pick, gather_scales("es_pick", es_table, adk_t[:], "rs2"))
        strict = sb.tile([P, LIST], F32, name="strict", tag="sq2")
        nc.scalar.activation(strict[:], mth_t[:].indirect(adk_t[:]), ACT.Copy)

        hid = [hidden(h, sat_t[h]) for h in range(2)]
        sc = [score(h, hid[h]) for h in range(2)]
        excl = [exclude(h, sc[h]) for h in range(2)]
        broad = [broader(h, excl[h]) for h in range(2)]
        xm = [scaled(0, excl[0], nc.vector), scaled(1, excl[1], nc.vector)]
        finish(0, xm[0], broad[0], halves)
        finish(1, xm[1], broad[1], halves)
